import numpy as np, ml_dtypes
CORES = [4,20,36,52,68,84,100,116,132,148,164,180,196,212,228,244]
N = 16
S, B = 2, 512
def setup_inputs(rng):
    a = (rng.standard_normal((128, 128), dtype=np.float32) / 8).astype(ml_dtypes.bfloat16)
    return {"x": (rng.standard_normal((N, 128, S * B), dtype=np.float32) / 2).astype(ml_dtypes.bfloat16), "a": np.broadcast_to(a, (N, 128, 128)).copy()}
def reference(x, a):
    X, A = x.astype(np.float64), a.astype(np.float64)
    y = np.zeros((N, 128, S * B)); h = np.zeros((128, B))
    for r in range(N):
        for s in range(S):
            h = np.tanh(A[r].T @ h + X[r][:, B * s:B * s + B])
            y[r][:, B * s:B * s + B] = h
    return {"y": y.astype(ml_dtypes.bfloat16)}

@@ -1,0 +1,134 @@
+from concourse.bass import DstId, RemoteDMATransfer
+from concourse.mybir import AluOpType, ActivationFunctionType
+
+N, S, B = 16, 2, 512
+G = 1
+n = N // G
+W = B // n
+TG = S * n
+NBK = 8
+RET = [(0, 4), (4, 8), (8, 12), (12, 16)]
+
+SCRATCH = {
+    "xin": ("sbuf", [128, TG, W], "bfloat16"),
+    "xs": ("sbuf", [128, TG, W], "bfloat16"),
+    "xl": ("sbuf", [128, TG, W], "bfloat16"),
+    "hb": ("sbuf", [128, TG, W], "bfloat16"),
+    "hin": ("sbuf", [128, W], "bfloat16"),
+    "yl": ("sbuf", [128, TG, W], "bfloat16"),
+    "yo": ("sbuf", [128, TG, W], "bfloat16"),
+    "a_sb": ("sbuf", [128, 128], "bfloat16"),
+    "ident": ("sbuf", [128, 128], "bfloat16"),
+    "acc": ("psum", [128, NBK, 512], "float32"),
+}
+SEMAPHORES = (["ld0", "ld1", "lda", "idm", "idn", "rl0", "rl1", "own", "hi", "ls", "ya", "rs0", "rs1", "st", "hs", "ms"]
+              + ["xa%d" % q for q in range(n)])
+
+
+def rank_program(g, core, T, topo):
+    me = T.rank_of(core)
+    if me is None:
+        return
+    sem = T.sem
+    gi, i = me // n, me % n
+    peer = [T.cores[gi * n + q] for q in range(n)]
+    v, te, sc, sy = g.vector, g.tensor, g.scalar, g.sync
+    hn = n // 2
+    ne = bin(topo.mask(core, peer[i - 1])).count("1")
+    ex = ne // hn
+
+    def write(dst, nth, width, src, out, rsem):
+        rid, pid = topo.addr(dst, core)
+        m = topo.mask(core, dst)
+        bits = [1 << b for b in range(m.bit_length()) if (m >> b) & 1][nth * width:(nth + 1) * width]
+        return RemoteDMATransfer(dst_ids=[DstId(rid=rid, pnc=pid)], dma_engine_mask=sum(bits), remote_sem=rsem,
+                                 src=src, dst=out)
+
+    first = (i // 2) % 2
+    order = [first, 1 - first]
+
+    for k, h in enumerate(order):
+        for s, q in ((0, sy), (1, sc)):
+            q.dma_start(T.xin[:, s * n + h * hn:s * n + (h + 1) * hn, :],
+                        T.x[:, B * s + W * hn * h:B * s + W * hn * (h + 1)]).then_inc(sem["ld%d" % k], 16)
+    sy.dma_start(T.a_sb[:], T.a[:]).then_inc(sem.lda, 16)
+
+    v.memset(T.ident[:], 1.0).then_inc(sem.idm, 1)
+    for k, h in enumerate(order):
+        v.wait_ge(sem["ld%d" % k], 32)
+        for s in range(S):
+            v.tensor_copy(T.xs[:, 2 * h * hn + s:2 * (h + 1) * hn:2, :],
+                          T.xin[:, s * n + h * hn:s * n + (h + 1) * hn, :]).then_inc(sem["rl%d" % k], 1)
+        if i // hn == h:
+            v.tensor_copy(T.xl[:, 2 * i:2 * i + 2, :], T.xin[:, i::n, :]).then_inc(sem.own, 1)
+
+    g.wait_ge(sem.idm, 1)
+    g.affine_select(T.ident[:], T.ident[:], [[-1, 128]], AluOpType.is_equal, 0.0, 0, 1).then_inc(sem.idn, 1)
+    left = 0
+    for k, h in enumerate(order):
+        g.wait_ge(sem["rl%d" % k], 2)
+        trs = [write(peer[j], j - h * hn, ex, T.xs[:, 2 * j:2 * j + 2, :], T.xl[:, 2 * i:2 * i + 2, :], sem["xa%d" % i])
+               for j in range(h * hn, (h + 1) * hn) if j != i]
+        g.remote_dma_fused(trs, local_sem=sem.ls)
+        left += ex * len(trs)
+
+    def hloc(tau):
+        return T.yl[:, tau, :] if tau // 2 == i else T.hb[:, tau, :]
+
+    def wait_x(queue, tau):
+        if tau // 2 == i:
+            queue.wait_ge(sem.own, 1)
+        else:
+            queue.wait_ge(sem["xa%d" % (tau // 2)], ex)
+
+    def open_group(tau):
+        wait_x(te, tau)
+        te.matmul(T.acc[:, tau % NBK, 0:W], T.ident[:], T.xl[:, tau, :], True, False)
+
+    t0 = 1 if gi == 0 else 0
+    te.wait_ge(sem.lda, 16)
+    te.wait_ge(sem.idn, 1)
+    for tau in range(t0, t0 + NBK):
+        open_group(tau)
+    opened = t0 + NBK
+    for tau in range(t0, TG):
+        if tau == 0:
+            te.wait_ge(sem.hi, ne)
+        else:
+            te.wait_ge(sem.hs, tau)
+        te.matmul(T.acc[:, tau % NBK, 0:W], T.a_sb[:], hloc(tau - 1) if tau > 0 else T.hin[:],
+                  False, True).then_inc(sem.ms, 1)
+        if opened < TG and opened - NBK < tau:
+            open_group(opened)
+            opened += 1
+
+    for tau in range(TG):
+        if tau < t0:
+            wait_x(sc, 0)
+            src = T.xl[:, 0, :]
+        else:
+            sc.wait_ge(sem.ms, tau - t0 + 1)
+            src = T.acc[:, tau % NBK, 0:W]
+        sc.activation(hloc(tau), src, ActivationFunctionType.Tanh).then_inc(sem.hs, 1)
+
+    for q0, q1 in RET:
+        e = ne // (q1 - q0)
+        g.wait_ge(sem.hs, 2 * q1)
+        if q1 == n and gi < G - 1:
+            g.remote_dma_fused([write(T.cores[me + n], 0, ne, hloc(TG - 1), T.hin[:], sem.hi)], local_sem=sem.ls)
+            left += ne
+        trs = [write(peer[q], q - q0, e, T.hb[:, 2 * q:2 * q + 2, :], T.yl[:, 2 * i:2 * i + 2, :], sem.ya)
+               for q in range(q0, q1) if q != i]
+        if trs:
+            g.remote_dma_fused(trs, local_sem=sem.ls)
+            left += e * len(trs)
+    g.wait_ge(sem.ls, left)
+
+    mine = [ne // (q1 - q0) for q0, q1 in RET if q0 <= i < q1][0]
+    v.wait_ge(sem.ya, mine * (n - 1))
+    v.wait_ge(sem.hs, 2 * i + 2)
+    for s in range(S):
+        v.tensor_copy(T.yo[:, s * n:(s + 1) * n, :], T.yl[:, s::2, :]).then_inc(sem["rs%d" % s], 1)
+        sy.wait_ge(sem["rs%d" % s], 1)
+        sy.dma_start(T.y[:, B * s:B * (s + 1)], T.yo[:, s * n:(s + 1) * n, :]).then_inc(sem.st, 16)
+    sy.wait_ge(sem.st, 32)

@@ -1,52 +1,59 @@
 from concourse.bass import DstId, RemoteDMATransfer
 from concourse.mybir import AluOpType, ActivationFunctionType
 
-N, S, B = 16, 2, 512
-G = 1
-n = N // G
+n, S, B = 16, 2, 512
 W = B // n
 TG = S * n
 NBK = 8
-RET = [(0, 4), (4, 8), (8, 12), (12, 16)]
+WAVE1 = [3, 2, 2]
+BLOCKS = [(0, 4), (4, 8), (8, 12)]
+DIRECT = [[24, 25, 26, 27], [28, 29], [30], [31]]
+Q0 = 12
 
 SCRATCH = {
+    "xq": ("sbuf", [128, S, W], "bfloat16"),
     "xin": ("sbuf", [128, TG, W], "bfloat16"),
     "xs": ("sbuf", [128, TG, W], "bfloat16"),
     "xl": ("sbuf", [128, TG, W], "bfloat16"),
     "hb": ("sbuf", [128, TG, W], "bfloat16"),
-    "hin": ("sbuf", [128, W], "bfloat16"),
     "yl": ("sbuf", [128, TG, W], "bfloat16"),
     "yo": ("sbuf", [128, TG, W], "bfloat16"),
     "a_sb": ("sbuf", [128, 128], "bfloat16"),
     "ident": ("sbuf", [128, 128], "bfloat16"),
     "acc": ("psum", [128, NBK, 512], "float32"),
 }
-SEMAPHORES = (["ld0", "ld1", "lda", "idm", "idn", "rl0", "rl1", "own", "hi", "ls", "ya", "rs0", "rs1", "st", "hs", "ms"]
-              + ["xa%d" % q for q in range(n)])
+SEMAPHORES = (["ldq", "ld0", "ld1", "lda", "idm", "idn", "rl0", "rl1", "own", "ls", "ya", "yd0", "yd1", "rs0", "rs1", "st",
+               "hs", "ms"] + ["xa%d" % q for q in range(n)])
 
 
 def rank_program(g, core, T, topo):
-    me = T.rank_of(core)
-    if me is None:
+    i = T.rank_of(core)
+    if i is None:
         return
     sem = T.sem
-    gi, i = me // n, me % n
-    peer = [T.cores[gi * n + q] for q in range(n)]
+    peer = T.cores
     v, te, sc, sy = g.vector, g.tensor, g.scalar, g.sync
-    hn = n // 2
     ne = bin(topo.mask(core, peer[i - 1])).count("1")
-    ex = ne // hn
+    hn = ne
+    left = [0]
 
     def write(dst, nth, width, src, out, rsem):
         rid, pid = topo.addr(dst, core)
         m = topo.mask(core, dst)
         bits = [1 << b for b in range(m.bit_length()) if (m >> b) & 1][nth * width:(nth + 1) * width]
+        left[0] += width
         return RemoteDMATransfer(dst_ids=[DstId(rid=rid, pnc=pid)], dma_engine_mask=sum(bits), remote_sem=rsem,
                                  src=src, dst=out)
 
+    def xwrite(j, src):
+        return write(peer[j], j % hn, 1, src, T.xl[:, 2 * i:2 * i + 2, :], sem["xa%d" % i])
+
     first = (i // 2) % 2
     order = [first, 1 - first]
+    jq = (i + hn) % n
 
+    for s, q in ((0, sy), (1, sc)):
+        q.dma_start(T.xq[:, s, :], T.x[:, B * s + W * jq:B * s + W * (jq + 1)]).then_inc(sem.ldq, 16)
     for k, h in enumerate(order):
         for s, q in ((0, sy), (1, sc)):
             q.dma_start(T.xin[:, s * n + h * hn:s * n + (h + 1) * hn, :],
@@ -64,71 +71,72 @@ def rank_program(g, core, T, topo):
 
     g.wait_ge(sem.idm, 1)
     g.affine_select(T.ident[:], T.ident[:], [[-1, 128]], AluOpType.is_equal, 0.0, 0, 1).then_inc(sem.idn, 1)
-    left = 0
+    g.wait_ge(sem.ldq, 32)
+    g.remote_dma_fused([xwrite(jq, T.xq[:, :, :])], local_sem=sem.ls)
     for k, h in enumerate(order):
         g.wait_ge(sem["rl%d" % k], 2)
-        trs = [write(peer[j], j - h * hn, ex, T.xs[:, 2 * j:2 * j + 2, :], T.xl[:, 2 * i:2 * i + 2, :], sem["xa%d" % i])
-               for j in range(h * hn, (h + 1) * hn) if j != i]
-        g.remote_dma_fused(trs, local_sem=sem.ls)
-        left += ex * len(trs)
+        trs = [xwrite(j, T.xs[:, 2 * j:2 * j + 2, :]) for j in range(h * hn, (h + 1) * hn) if j != i and j != jq]
+        for m in (WAVE1 if k == 0 else [len(trs)]):
+            g.remote_dma_fused(trs[:m], local_sem=sem.ls)
+            trs = trs[m:]
 
     def hloc(tau):
-        return T.yl[:, tau, :] if tau // 2 == i else T.hb[:, tau, :]
+        if tau // 2 != i:
+            return T.hb[:, tau, :]
+        return T.yo[:, (tau % 2) * n + i, :] if i >= Q0 else T.yl[:, tau, :]
 
     def wait_x(queue, tau):
         if tau // 2 == i:
             queue.wait_ge(sem.own, 1)
         else:
-            queue.wait_ge(sem["xa%d" % (tau // 2)], ex)
+            queue.wait_ge(sem["xa%d" % (tau // 2)], 1)
 
     def open_group(tau):
         wait_x(te, tau)
         te.matmul(T.acc[:, tau % NBK, 0:W], T.ident[:], T.xl[:, tau, :], True, False)
 
-    t0 = 1 if gi == 0 else 0
     te.wait_ge(sem.lda, 16)
     te.wait_ge(sem.idn, 1)
-    for tau in range(t0, t0 + NBK):
+    for tau in range(1, 1 + NBK):
         open_group(tau)
-    opened = t0 + NBK
-    for tau in range(t0, TG):
-        if tau == 0:
-            te.wait_ge(sem.hi, ne)
-        else:
-            te.wait_ge(sem.hs, tau)
-        te.matmul(T.acc[:, tau % NBK, 0:W], T.a_sb[:], hloc(tau - 1) if tau > 0 else T.hin[:],
-                  False, True).then_inc(sem.ms, 1)
+    opened = 1 + NBK
+    for tau in range(1, TG):
+        te.wait_ge(sem.hs, tau)
+        te.matmul(T.acc[:, tau % NBK, 0:W], T.a_sb[:], hloc(tau - 1), False, True).then_inc(sem.ms, 1)
         if opened < TG and opened - NBK < tau:
             open_group(opened)
             opened += 1
 
-    for tau in range(TG):
-        if tau < t0:
-            wait_x(sc, 0)
-            src = T.xl[:, 0, :]
-        else:
-            sc.wait_ge(sem.ms, tau - t0 + 1)
-            src = T.acc[:, tau % NBK, 0:W]
-        sc.activation(hloc(tau), src, ActivationFunctionType.Tanh).then_inc(sem.hs, 1)
+    wait_x(sc, 0)
+    sc.activation(hloc(0), T.xl[:, 0, :], ActivationFunctionType.Tanh).then_inc(sem.hs, 1)
+    for tau in range(1, TG):
+        sc.wait_ge(sem.ms, tau)
+        sc.activation(hloc(tau), T.acc[:, tau % NBK, 0:W], ActivationFunctionType.Tanh).then_inc(sem.hs, 1)
 
-    for q0, q1 in RET:
-        e = ne // (q1 - q0)
+    for q0, q1 in BLOCKS:
         g.wait_ge(sem.hs, 2 * q1)
-        if q1 == n and gi < G - 1:
-            g.remote_dma_fused([write(T.cores[me + n], 0, ne, hloc(TG - 1), T.hin[:], sem.hi)], local_sem=sem.ls)
-            left += ne
-        trs = [write(peer[q], q - q0, e, T.hb[:, 2 * q:2 * q + 2, :], T.yl[:, 2 * i:2 * i + 2, :], sem.ya)
+        trs = [write(peer[q], q - q0, ne // (q1 - q0), T.hb[:, 2 * q:2 * q + 2, :], T.yl[:, 2 * i:2 * i + 2, :], sem.ya)
                for q in range(q0, q1) if q != i]
+        g.remote_dma_fused(trs, local_sem=sem.ls)
+    for ts in DIRECT:
+        g.wait_ge(sem.hs, ts[-1] + 1)
+        trs = [write(peer[t // 2], k, ne // len(ts), T.hb[:, t, :], T.yo[:, (t % 2) * n + i, :], sem["yd%d" % (t % 2)])
+               for k, t in enumerate(ts) if t // 2 != i]
         if trs:
             g.remote_dma_fused(trs, local_sem=sem.ls)
-            left += e * len(trs)
-    g.wait_ge(sem.ls, left)
+    g.wait_ge(sem.ls, left[0])
 
-    mine = [ne // (q1 - q0) for q0, q1 in RET if q0 <= i < q1][0]
-    v.wait_ge(sem.ya, mine * (n - 1))
-    v.wait_ge(sem.hs, 2 * i + 2)
+    if i < Q0:
+        mine = [ne // (q1 - q0) for q0, q1 in BLOCKS if q0 <= i < q1][0]
+        v.wait_ge(sem.ya, mine * (n - 1))
+        v.wait_ge(sem.hs, 2 * i + 2)
     for s in range(S):
-        v.tensor_copy(T.yo[:, s * n:(s + 1) * n, :], T.yl[:, s::2, :]).then_inc(sem["rs%d" % s], 1)
-        sy.wait_ge(sem["rs%d" % s], 1)
+        if i < Q0:
+            v.tensor_copy(T.yo[:, s * n:(s + 1) * n, :], T.yl[:, s::2, :]).then_inc(sem["rs%d" % s], 1)
+            sy.wait_ge(sem["rs%d" % s], 1)
+        else:
+            mine = [ne // len(ts) for ts in DIRECT if 2 * i + s in ts][0]
+            sy.wait_ge(sem["yd%d" % s], mine * (n - 1))
+            sy.wait_ge(sem.hs, 2 * i + s + 1)
         sy.dma_start(T.y[:, B * s:B * (s + 1)], T.yo[:, s * n:(s + 1) * n, :]).then_inc(sem.st, 16)
     sy.wait_ge(sem.st, 32)

from concourse.bass import DstId, RemoteDMATransfer
from concourse.mybir import AluOpType, ActivationFunctionType

n, S, B = 16, 2, 512
W = B // n
TG = S * n
NBK = 8
WAVE1 = [3, 2, 2]
BLOCKS = [(0, 4), (4, 8), (8, 12)]
DIRECT = [[24, 25, 26, 27], [28, 29], [30], [31]]
Q0 = 12

SCRATCH = {
    "xq": ("sbuf", [128, S, W], "bfloat16"),
    "xin": ("sbuf", [128, TG, W], "bfloat16"),
    "xs": ("sbuf", [128, TG, W], "bfloat16"),
    "xl": ("sbuf", [128, TG, W], "bfloat16"),
    "hb": ("sbuf", [128, TG, W], "bfloat16"),
    "yl": ("sbuf", [128, TG, W], "bfloat16"),
    "yo": ("sbuf", [128, TG, W], "bfloat16"),
    "a_sb": ("sbuf", [128, 128], "bfloat16"),
    "ident": ("sbuf", [128, 128], "bfloat16"),
    "acc": ("psum", [128, NBK, 512], "float32"),
}
SEMAPHORES = (["ldq", "ld0", "ld1", "lda", "idm", "idn", "rl0", "rl1", "own", "ls", "ya", "yd0", "yd1", "rs0", "rs1", "st",
               "hs", "ms"] + ["xa%d" % q for q in range(n)])


def rank_program(g, core, T, topo):
    i = T.rank_of(core)
    if i is None:
        return
    sem = T.sem
    peer = T.cores
    v, te, sc, sy = g.vector, g.tensor, g.scalar, g.sync
    ne = bin(topo.mask(core, peer[i - 1])).count("1")
    hn = ne
    left = [0]

    def write(dst, nth, width, src, out, rsem):
        rid, pid = topo.addr(dst, core)
        m = topo.mask(core, dst)
        bits = [1 << b for b in range(m.bit_length()) if (m >> b) & 1][nth * width:(nth + 1) * width]
        left[0] += width
        return RemoteDMATransfer(dst_ids=[DstId(rid=rid, pnc=pid)], dma_engine_mask=sum(bits), remote_sem=rsem,
                                 src=src, dst=out)

    def xwrite(j, src):
        return write(peer[j], j % hn, 1, src, T.xl[:, 2 * i:2 * i + 2, :], sem["xa%d" % i])

    first = (i // 2) % 2
    order = [first, 1 - first]
    jq = (i + hn) % n

    for s, q in ((0, sy), (1, sc)):
        q.dma_start(T.xq[:, s, :], T.x[:, B * s + W * jq:B * s + W * (jq + 1)]).then_inc(sem.ldq, 16)
    for k, h in enumerate(order):
        for s, q in ((0, sy), (1, sc)):
            q.dma_start(T.xin[:, s * n + h * hn:s * n + (h + 1) * hn, :],
                        T.x[:, B * s + W * hn * h:B * s + W * hn * (h + 1)]).then_inc(sem["ld%d" % k], 16)
    sy.dma_start(T.a_sb[:], T.a[:]).then_inc(sem.lda, 16)

    v.memset(T.ident[:], 1.0).then_inc(sem.idm, 1)
    for k, h in enumerate(order):
        v.wait_ge(sem["ld%d" % k], 32)
        for s in range(S):
            v.tensor_copy(T.xs[:, 2 * h * hn + s:2 * (h + 1) * hn:2, :],
                          T.xin[:, s * n + h * hn:s * n + (h + 1) * hn, :]).then_inc(sem["rl%d" % k], 1)
        if i // hn == h:
            v.tensor_copy(T.xl[:, 2 * i:2 * i + 2, :], T.xin[:, i::n, :]).then_inc(sem.own, 1)

    g.wait_ge(sem.idm, 1)
    g.affine_select(T.ident[:], T.ident[:], [[-1, 128]], AluOpType.is_equal, 0.0, 0, 1).then_inc(sem.idn, 1)
    g.wait_ge(sem.ldq, 32)
    g.remote_dma_fused([xwrite(jq, T.xq[:, :, :])], local_sem=sem.ls)
    for k, h in enumerate(order):
        g.wait_ge(sem["rl%d" % k], 2)
        trs = [xwrite(j, T.xs[:, 2 * j:2 * j + 2, :]) for j in range(h * hn, (h + 1) * hn) if j != i and j != jq]
        for m in (WAVE1 if k == 0 else [len(trs)]):
            g.remote_dma_fused(trs[:m], local_sem=sem.ls)
            trs = trs[m:]

    def hloc(tau):
        if tau // 2 != i:
            return T.hb[:, tau, :]
        return T.yo[:, (tau % 2) * n + i, :] if i >= Q0 else T.yl[:, tau, :]

    def wait_x(queue, tau):
        if tau // 2 == i:
            queue.wait_ge(sem.own, 1)
        else:
            queue.wait_ge(sem["xa%d" % (tau // 2)], 1)

    def open_group(tau):
        wait_x(te, tau)
        te.matmul(T.acc[:, tau % NBK, 0:W], T.ident[:], T.xl[:, tau, :], True, False)

    te.wait_ge(sem.lda, 16)
    te.wait_ge(sem.idn, 1)
    for tau in range(1, 1 + NBK):
        open_group(tau)
    opened = 1 + NBK
    for tau in range(1, TG):
        te.wait_ge(sem.hs, tau)
        te.matmul(T.acc[:, tau % NBK, 0:W], T.a_sb[:], hloc(tau - 1), False, True).then_inc(sem.ms, 1)
        if opened < TG and opened - NBK < tau:
            open_group(opened)
            opened += 1

    wait_x(sc, 0)
    sc.activation(hloc(0), T.xl[:, 0, :], ActivationFunctionType.Tanh).then_inc(sem.hs, 1)
    for tau in range(1, TG):
        sc.wait_ge(sem.ms, tau)
        sc.activation(hloc(tau), T.acc[:, tau % NBK, 0:W], ActivationFunctionType.Tanh).then_inc(sem.hs, 1)

    for q0, q1 in BLOCKS:
        g.wait_ge(sem.hs, 2 * q1)
        trs = [write(peer[q], q - q0, ne // (q1 - q0), T.hb[:, 2 * q:2 * q + 2, :], T.yl[:, 2 * i:2 * i + 2, :], sem.ya)
               for q in range(q0, q1) if q != i]
        g.remote_dma_fused(trs, local_sem=sem.ls)
    for ts in DIRECT:
        g.wait_ge(sem.hs, ts[-1] + 1)
        trs = [write(peer[t // 2], k, ne // len(ts), T.hb[:, t, :], T.yo[:, (t % 2) * n + i, :], sem["yd%d" % (t % 2)])
               for k, t in enumerate(ts) if t // 2 != i]
        if trs:
            g.remote_dma_fused(trs, local_sem=sem.ls)
    g.wait_ge(sem.ls, left[0])

    if i < Q0:
        mine = [ne // (q1 - q0) for q0, q1 in BLOCKS if q0 <= i < q1][0]
        v.wait_ge(sem.ya, mine * (n - 1))
        v.wait_ge(sem.hs, 2 * i + 2)
    for s in range(S):
        if i < Q0:
            v.tensor_copy(T.yo[:, s * n:(s + 1) * n, :], T.yl[:, s::2, :]).then_inc(sem["rs%d" % s], 1)
            sy.wait_ge(sem["rs%d" % s], 1)
        else:
            mine = [ne // len(ts) for ts in DIRECT if 2 * i + s in ts][0]
            sy.wait_ge(sem["yd%d" % s], mine * (n - 1))
            sy.wait_ge(sem.hs, 2 * i + s + 1)
        sy.dma_start(T.y[:, B * s:B * (s + 1)], T.yo[:, s * n:(s + 1) * n, :]).then_inc(sem.st, 16)
    sy.wait_ge(sem.st, 32)
